import numpy as np
import ml_dtypes


def mxq(x, axis, fmt="e4m3"):
    dtype, down = {"e4m3": (ml_dtypes.float8_e4m3fn, 7), "e5m2": (ml_dtypes.float8_e5m2, 14)}[fmt]
    v = np.moveaxis(np.asarray(x, np.float32).astype(ml_dtypes.bfloat16).astype(np.float64), axis, -1)
    blocks = v.reshape(v.shape[:-1] + (-1, 32))
    amax = np.abs(blocks).max(-1, keepdims=True)
    byte = np.maximum(np.where(amax > 0, np.frexp(amax)[1] - 1 + 127, 0) - down, 1)
    scale = np.exp2(byte - 127.0)
    codes = (blocks / scale).astype(np.float32).astype(dtype).astype(np.float64)
    return np.moveaxis((codes * scale).reshape(v.shape), -1, axis)


WIDE = False


def mx_kscale(k):
    if not WIDE:
        return np.ones(k)
    levels = np.array([10, -10, 5, -5, 0])
    if k % 512:
        return np.exp2(np.random.permutation(np.resize(levels, k // 32))).repeat(32)
    a = np.empty((k // 512, 16))
    for p in range(k // 512):
        a[p, :8] = np.random.permutation(np.resize(levels, 8))
        for g in range(8):
            far = levels[np.abs(levels - a[p, g]) >= 10]
            a[p, g + 8] = far[np.random.randint(len(far))]
    return np.exp2(a.ravel()).repeat(32)


def f64(x):
    return np.asarray(x).astype(np.float64)


def striped(idx):
    return np.tile(np.asarray(idx).reshape(-1, 16).T, (8, 1)).astype(np.uint16)


def unstriped(offs):
    return offs[:16].T.reshape(-1).astype(np.int64)


E2M1 = np.array([0.0, 0.5, 1.0, 1.5, 2.0, 3.0, 4.0, 6.0, -0.0, -0.5, -1.0, -1.5, -2.0, -3.0, -4.0, -6.0])


def pack_weight(w, fmt):
    k, n = w.shape
    w = f64(np.asarray(w, np.float32).astype(ml_dtypes.bfloat16)).reshape(k // 32, 32, n)
    amax = np.abs(w).max(1)
    if fmt == "e4m3":
        byte = np.frexp(amax)[1] - 1 + 127 - 7
    else:
        mant, ex = np.frexp(amax / 6.0)
        byte = np.where(mant > 0.5, ex, ex - 1) + 127
    byte = np.clip(np.where(amax > 0, byte, 1), 1, 254)
    scaled = (w * np.exp2(127.0 - byte)[:, None, :]).reshape(k, n).astype(np.float32)
    by_word = np.ascontiguousarray(scaled.reshape(k // 512, 128, 4, n).transpose(0, 1, 3, 2))
    if fmt == "e4m3":
        words = by_word.astype(ml_dtypes.float8_e4m3fn).view(np.uint8)
    else:
        c = by_word.astype(ml_dtypes.float4_e2m1fn).view(np.uint8) & 0xF
        words = (c[..., 0::2] | (c[..., 1::2] << 4)).reshape(k // 512, 128, 2 * n)
    return np.ascontiguousarray(words), np.ascontiguousarray(byte.astype(np.uint8).reshape(k // 512, 16, n))


def unpack_weight(words, scales, fmt):
    g, _, n = scales.shape
    words = np.ascontiguousarray(words).reshape(g, 128, n, -1)
    if fmt == "e4m3":
        vals = words.view(ml_dtypes.float8_e4m3fn).astype(np.float64)
    else:
        nib = np.empty((g, 128, n, 4), np.uint8)
        nib[..., 0::2] = words & 0xF
        nib[..., 1::2] = words >> 4
        vals = E2M1[nib]
    vals = vals * np.repeat(np.exp2(scales.astype(np.float64) - 127.0), 8, axis=1)[..., None]
    return vals.transpose(0, 1, 3, 2).reshape(g * 512, n)


B, N, T, D, NQ = 1, 512, 2048, 512, 512
SEG = 32


def setup_inputs():
    n = np.random.standard_normal
    idx = np.random.permutation(T)[:B * N]
    s = mx_kscale(D)[:, None]
    kp = pack_weight(n((D, T)) / s, "e4m3")
    return {
        "qT": (n((B, D, NQ)) * s * (1.00 / np.sqrt(D))).astype(np.float32),
        "k_words": kp[0],
        "k_scales": kp[1],
        "nb": np.tile(0.5 * n(2048), (128, 1)).astype(np.float32),
        "offs": striped(idx),
    }


def reference(qT, k_words, k_scales, nb, offs):
    idx = unstriped(offs)
    pick = lambda x, which: x[:, which].reshape(x.shape[0], B, -1).transpose(1, 0, 2)
    k = unpack_weight(k_words, k_scales, "e4m3")
    kg = pick(k, idx)
    qq = mxq(f64(qT), 1, "e4m3")
    a = kg.transpose(0, 2, 1) @ qq
    y = np.maximum(a + pick(f64(nb), idx)[:, :1, :].transpose(0, 2, 1), 0.0).reshape(B, N, NQ // SEG, SEG).mean(-1)
    return y

@@ -1,0 +1,117 @@
+from contextlib import ExitStack
+
+import concourse.mybir as mybir
+from concourse.masks import make_identity
+
+N, T, D, NQ, SEG = 512, 2048, 512, 512, 32
+FLOPS = 2 * N * D * NQ
+P = 128
+PACK = 4
+TILES = N // P
+RUNS = NQ // SEG
+
+F32 = mybir.dt.float32
+BF16 = mybir.dt.bfloat16
+I32 = mybir.dt.int32
+U32 = mybir.dt.uint32
+U16 = mybir.dt.uint16
+U8 = mybir.dt.uint8
+FP8X4 = mybir.dt.float8_e4m3fn_x4
+ACT = mybir.ActivationFunctionType
+ALU = mybir.AluOpType
+AX = mybir.AxisListType
+
+BIAS_ROW = P - 1
+PIECES = [(0, 0, 256), (0, 256, 256), (1, 0, 512), (2, 0, 512), (3, 0, 256), (3, 256, 256)]
+
+
+def tile_attend_tok_meanact_topk_kernel(tc, qT, k_words, k_scales, nb, offs, out):
+    nc = tc.nc
+    with ExitStack() as ctx:
+        keep = ctx.enter_context(tc.tile_pool(name="keep", bufs=1))
+        psum = ctx.enter_context(tc.psum_pool(name="psum", bufs=1))
+
+        offsets = keep.tile([P, N // 16], U16, name="offsets")
+        nc.sync.dma_start(offsets[:], offs)
+
+        scale_pool = keep.tile([P, T // 4], I32, name="scale_pool", align_bytes=64)
+        nc.vector.memset(scale_pool[:], 0)
+        bias_pool = keep.tile([P, T], F32, name="bias_pool", align_bytes=64)
+        nc.vector.memset(bias_pool[0:BIAS_ROW, :], 0.0)
+        nc.scalar.dma_start(out=bias_pool[BIAS_ROW:P, :], in_=nb[0:1, :])
+        scale_rows = k_scales[0].bitcast(I32)
+        for quad in range(4):
+            queue = nc.sync if quad < 2 else nc.scalar
+            queue.dma_start(out=scale_pool[32 * quad : 32 * quad + 4, :], in_=scale_rows[4 * quad : 4 * quad + 4, :])
+
+        q_raw = keep.tile([P, PACK, NQ], F32, name="q_raw", align_bytes=64)
+        nc.sync.dma_start(out=q_raw[:], in_=qT[0].rearrange("(p j) w -> p j w", j=PACK))
+        word_pool = keep.tile([P, T], I32, name="word_pool", align_bytes=64)
+        nc.sync.dma_start(out=word_pool[:], in_=k_words[0].rearrange("p n t -> p (n t)").bitcast(I32))
+
+
+        ident_raw = keep.tile([P, P], F32, name="ident_raw", align_bytes=64)
+        make_identity(nc, ident_raw[:])
+        ident = keep.tile([P, P], F32, name="ident", align_bytes=64)
+        nc.scalar.activation(out=ident[:], in_=ident_raw[:], func=ACT.Relu)
+
+        bias_rows = keep.tile([P, N], F32, name="bias_rows", align_bytes=64)
+        nc.vector.tensor_copy(out=bias_rows[:], in_=bias_pool[:].indirect(offsets[:]))
+        k_scale = keep.tile([P, N], U8, name="k_scale", align_bytes=64)
+        nc.vector.tensor_copy(out=k_scale[:], in_=scale_pool[:].bitcast(U8).indirect(offsets[:]))
+
+        bias_turned = psum.tile([P, TILES, P], F32, name="bias_turned")
+        for m in range(TILES):
+            nc.tensor.transpose(bias_turned[:, m, :], bias_rows[:, m * P : (m + 1) * P], ident[:])
+
+        q_grouped = keep.tile([P, NQ, PACK], BF16, name="q_grouped", align_bytes=64)
+        half = NQ // 2
+        dst = lambda c0: q_grouped[:, c0 : c0 + half, :].rearrange("p (c i) t -> p c t i", i=4)
+        src = lambda c0: q_raw[:, :, c0 : c0 + half].rearrange("p t (c i) -> p c t i", i=4)
+        nc.scalar.copy(out=dst(0), in_=src(0))
+        nc.vector.tensor_copy(out=dst(half), in_=src(half))
+
+        bias = keep.tile([P, TILES], F32, name="bias", align_bytes=64)
+        nc.scalar.activation(out=bias[:], in_=bias_turned[:, :, BIAS_ROW], func=ACT.Copy, scale=1.0 / SEG)
+
+        q_code = keep.tile([P, NQ], U32, name="q_code", align_bytes=64)
+        q_scale = keep.tile([P, NQ], U8, name="q_scale", align_bytes=64)
+        for c0 in (0, half):
+            nc.vector.quantize_mx(
+                out=q_code[:, c0 : c0 + half].bitcast(FP8X4),
+                scales=q_scale[:, c0 : c0 + half],
+                in_=q_grouped[:, c0 : c0 + half, :].rearrange("p w t -> p (w t)"),
+            )
+
+        k_code = keep.tile([P, N], U32, name="k_code", align_bytes=64)
+        for h in range(2):
+            nc.vector.tensor_copy(
+                out=k_code[:, h * 256 : (h + 1) * 256],
+                in_=word_pool[:].bitcast(U32).indirect(offsets[:, h * 16 : (h + 1) * 16]),
+            )
+
+        active = keep.tile([P, TILES, NQ], F32, name="active", align_bytes=64)
+        means = keep.tile([P, TILES, RUNS], F32, name="means", align_bytes=64)
+        out_view = out[0].rearrange("(m p) j -> p m j", p=P)
+        for index, (m, c0, width) in enumerate(PIECES):
+            acc = psum.tile([P, width], F32, name="acc%d" % index)
+            nc.tensor.matmul_mx(
+                out=acc[:],
+                lhsT=k_code[:, m * P : (m + 1) * P].bitcast(FP8X4),
+                lhsT_scale=k_scale[:, m * P : (m + 1) * P],
+                rhs=q_code[:, c0 : c0 + width].bitcast(FP8X4),
+                rhs_scale=q_scale[:, c0 : c0 + width],
+                start=True,
+                stop=True,
+            )
+            nc.scalar.activation(
+                out=active[:, m, c0 : c0 + width], in_=acc[:], func=ACT.Relu, bias=bias[:, m : m + 1], scale=1.0 / SEG
+            )
+            nc.vector.tensor_reduce(
+                out=means[:, m, c0 // SEG : (c0 + width) // SEG],
+                in_=active[:, m, c0 : c0 + width].rearrange("p (j e) -> p j e", e=SEG),
+                axis=AX.X,
+                op=ALU.add,
+            )
+            if c0 + width == NQ:
+                nc.sync.dma_start(out=out_view[:, m, :], in_=means[:, m, :])

@@ -22,7 +22,8 @@ ALU = mybir.AluOpType
 AX = mybir.AxisListType
 
 BIAS_ROW = P - 1
-PIECES = [(0, 0, 256), (0, 256, 256), (1, 0, 512), (2, 0, 512), (3, 0, 256), (3, 256, 256)]
+HALF = NQ // 2
+PIECES = [(m, c0, 256) for c0 in (0, 256) for m in range(TILES)]
 
 
 def tile_attend_tok_meanact_topk_kernel(tc, qT, k_words, k_scales, nb, offs, out):
@@ -38,17 +39,17 @@ def tile_attend_tok_meanact_topk_kernel(tc, qT, k_words, k_scales, nb, offs, out
         nc.vector.memset(scale_pool[:], 0)
         bias_pool = keep.tile([P, T], F32, name="bias_pool", align_bytes=64)
         nc.vector.memset(bias_pool[0:BIAS_ROW, :], 0.0)
-        nc.scalar.dma_start(out=bias_pool[BIAS_ROW:P, :], in_=nb[0:1, :])
+        nc.sync.dma_start(out=bias_pool[BIAS_ROW:P, :], in_=nb[0:1, :])
+
+        q_rows = qT[0].rearrange("(p j) w -> p j w", j=PACK)
+        q_raw = [keep.tile([P, PACK, HALF], F32, name="q_raw%d" % h, tag="stage%d" % h, align_bytes=64) for h in range(2)]
+        nc.sync.dma_start(out=q_raw[0][:], in_=q_rows[:, :, 0:HALF])
         scale_rows = k_scales[0].bitcast(I32)
         for quad in range(4):
-            queue = nc.sync if quad < 2 else nc.scalar
-            queue.dma_start(out=scale_pool[32 * quad : 32 * quad + 4, :], in_=scale_rows[4 * quad : 4 * quad + 4, :])
-
-        q_raw = keep.tile([P, PACK, NQ], F32, name="q_raw", align_bytes=64)
-        nc.sync.dma_start(out=q_raw[:], in_=qT[0].rearrange("(p j) w -> p j w", j=PACK))
+            nc.sync.dma_start(out=scale_pool[32 * quad : 32 * quad + 4, :], in_=scale_rows[4 * quad : 4 * quad + 4, :])
         word_pool = keep.tile([P, T], I32, name="word_pool", align_bytes=64)
         nc.sync.dma_start(out=word_pool[:], in_=k_words[0].rearrange("p n t -> p (n t)").bitcast(I32))
-
+        nc.sync.dma_start(out=q_raw[1][:], in_=q_rows[:, :, HALF:NQ])
 
         ident_raw = keep.tile([P, P], F32, name="ident_raw", align_bytes=64)
         make_identity(nc, ident_raw[:])
@@ -57,32 +58,33 @@ def tile_attend_tok_meanact_topk_kernel(tc, qT, k_words, k_scales, nb, offs, out
 
         bias_rows = keep.tile([P, N], F32, name="bias_rows", align_bytes=64)
         nc.vector.tensor_copy(out=bias_rows[:], in_=bias_pool[:].indirect(offsets[:]))
-        k_scale = keep.tile([P, N], U8, name="k_scale", align_bytes=64)
-        nc.vector.tensor_copy(out=k_scale[:], in_=scale_pool[:].bitcast(U8).indirect(offsets[:]))
-
-        bias_turned = psum.tile([P, TILES, P], F32, name="bias_turned")
+        bias_turned = psum.tile([P, TILES, P], F32, name="bias_turned", tag="bank7")
         for m in range(TILES):
             nc.tensor.transpose(bias_turned[:, m, :], bias_rows[:, m * P : (m + 1) * P], ident[:])
 
-        q_grouped = keep.tile([P, NQ, PACK], BF16, name="q_grouped", align_bytes=64)
-        half = NQ // 2
-        dst = lambda c0: q_grouped[:, c0 : c0 + half, :].rearrange("p (c i) t -> p c t i", i=4)
-        src = lambda c0: q_raw[:, :, c0 : c0 + half].rearrange("p t (c i) -> p c t i", i=4)
-        nc.scalar.copy(out=dst(0), in_=src(0))
-        nc.vector.tensor_copy(out=dst(half), in_=src(half))
+        q_code = keep.tile([P, NQ], U32, name="q_code", align_bytes=64)
+        q_scale = keep.tile([P, NQ], U8, name="q_scale", align_bytes=64)
+
+        def quantize_half(h):
+            grouped = keep.tile([P, HALF, PACK], BF16, name="q_grouped%d" % h, align_bytes=64)
+            share = HALF // 2
+            dst = lambda c0: grouped[:, c0 : c0 + share, :].rearrange("p (c i) t -> p c t i", i=4)
+            src = lambda c0: q_raw[h][:, :, c0 : c0 + share].rearrange("p t (c i) -> p c t i", i=4)
+            nc.scalar.copy(out=dst(0), in_=src(0))
+            nc.vector.tensor_copy(out=dst(share), in_=src(share))
+            nc.vector.quantize_mx(
+                out=q_code[:, h * HALF : (h + 1) * HALF].bitcast(FP8X4),
+                scales=q_scale[:, h * HALF : (h + 1) * HALF],
+                in_=grouped[:].rearrange("p w t -> p (w t)"),
+            )
+
+        quantize_half(0)
 
         bias = keep.tile([P, TILES], F32, name="bias", align_bytes=64)
         nc.scalar.activation(out=bias[:], in_=bias_turned[:, :, BIAS_ROW], func=ACT.Copy, scale=1.0 / SEG)
 
-        q_code = keep.tile([P, NQ], U32, name="q_code", align_bytes=64)
-        q_scale = keep.tile([P, NQ], U8, name="q_scale", align_bytes=64)
-        for c0 in (0, half):
-            nc.vector.quantize_mx(
-                out=q_code[:, c0 : c0 + half].bitcast(FP8X4),
-                scales=q_scale[:, c0 : c0 + half],
-                in_=q_grouped[:, c0 : c0 + half, :].rearrange("p w t -> p (w t)"),
-            )
-
+        k_scale = keep.tile([P, N], U8, name="k_scale", align_bytes=64)
+        nc.vector.tensor_copy(out=k_scale[:], in_=scale_pool[:].bitcast(U8).indirect(offsets[:]))
         k_code = keep.tile([P, N], U32, name="k_code", align_bytes=64)
         for h in range(2):
             nc.vector.tensor_copy(
@@ -90,11 +92,13 @@ def tile_attend_tok_meanact_topk_kernel(tc, qT, k_words, k_scales, nb, offs, out
                 in_=word_pool[:].bitcast(U32).indirect(offsets[:, h * 16 : (h + 1) * 16]),
             )
 
-        active = keep.tile([P, TILES, NQ], F32, name="active", align_bytes=64)
+        quantize_half(1)
+
+        active = keep.tile([P, TILES, NQ], F32, name="active", tag="stage1", align_bytes=64)
         means = keep.tile([P, TILES, RUNS], F32, name="means", align_bytes=64)
         out_view = out[0].rearrange("(m p) j -> p m j", p=P)
         for index, (m, c0, width) in enumerate(PIECES):
-            acc = psum.tile([P, width], F32, name="acc%d" % index)
+            acc = psum.tile([P, width], F32, name="acc%d" % index, tag="bank%d" % index)
             nc.tensor.matmul_mx(
                 out=acc[:],
                 lhsT=k_code[:, m * P : (m + 1) * P].bitcast(FP8X4),

@@ -35,7 +35,7 @@ def tile_attend_tok_meanact_topk_kernel(tc, qT, k_words, k_scales, nb, offs, out
         offsets = keep.tile([P, N // 16], U16, name="offsets")
         nc.sync.dma_start(offsets[:], offs)
 
-        scale_pool = keep.tile([P, T // 4], I32, name="scale_pool", align_bytes=64)
+        scale_pool = keep.tile([P, T // 4], I32, name="scale_pool", tag="scales_then_codes", align_bytes=64)
         nc.vector.memset(scale_pool[:], 0)
         bias_pool = keep.tile([P, T], F32, name="bias_pool", align_bytes=64)
         nc.vector.memset(bias_pool[0:BIAS_ROW, :], 0.0)
@@ -44,17 +44,15 @@ def tile_attend_tok_meanact_topk_kernel(tc, qT, k_words, k_scales, nb, offs, out
         q_rows = qT[0].rearrange("(p j) w -> p j w", j=PACK)
         q_raw = [keep.tile([P, PACK, HALF], F32, name="q_raw%d" % h, tag="stage%d" % h, align_bytes=64) for h in range(2)]
         nc.sync.dma_start(out=q_raw[0][:], in_=q_rows[:, :, 0:HALF])
-        scale_rows = k_scales[0].bitcast(I32)
-        for quad in range(4):
-            nc.sync.dma_start(out=scale_pool[32 * quad : 32 * quad + 4, :], in_=scale_rows[4 * quad : 4 * quad + 4, :])
+        nc.sync.dma_start(out=scale_pool[0:P:8, :], in_=k_scales[0].bitcast(I32))
+        k_scale_words = keep.tile([P, N // 4], I32, name="k_scale_words", align_bytes=64)
+        nc.vector.memset(k_scale_words[:], 0)
         word_pool = keep.tile([P, T], I32, name="word_pool", align_bytes=64)
         nc.sync.dma_start(out=word_pool[:], in_=k_words[0].rearrange("p n t -> p (n t)").bitcast(I32))
         nc.sync.dma_start(out=q_raw[1][:], in_=q_rows[:, :, HALF:NQ])
 
-        ident_raw = keep.tile([P, P], F32, name="ident_raw", align_bytes=64)
-        make_identity(nc, ident_raw[:])
         ident = keep.tile([P, P], F32, name="ident", align_bytes=64)
-        nc.scalar.activation(out=ident[:], in_=ident_raw[:], func=ACT.Relu)
+        make_identity(nc, ident[:])
 
         bias_rows = keep.tile([P, N], F32, name="bias_rows", align_bytes=64)
         nc.vector.tensor_copy(out=bias_rows[:], in_=bias_pool[:].indirect(offsets[:]))
@@ -62,29 +60,33 @@ def tile_attend_tok_meanact_topk_kernel(tc, qT, k_words, k_scales, nb, offs, out
         for m in range(TILES):
             nc.tensor.transpose(bias_turned[:, m, :], bias_rows[:, m * P : (m + 1) * P], ident[:])
 
-        q_code = keep.tile([P, NQ], U32, name="q_code", align_bytes=64)
+        scale_picked = keep.tile([P, N], U8, name="scale_picked", align_bytes=64)
+        nc.vector.tensor_copy(out=scale_picked[:], in_=scale_pool[:].bitcast(U8).indirect(offsets[:]))
+        for r in range(4):
+            nc.sync.dma_start(out=k_scale_words[r:P:32, :], in_=scale_picked[8 * r : P : 32, :].bitcast(I32))
+        k_scale = k_scale_words[:].bitcast(U8)
+
+        q_code = keep.tile([P, NQ], U32, name="q_code", tag="scales_then_codes", align_bytes=64)
         q_scale = keep.tile([P, NQ], U8, name="q_scale", align_bytes=64)
 
-        def quantize_half(h):
+        def quantize_half(h, share):
             grouped = keep.tile([P, HALF, PACK], BF16, name="q_grouped%d" % h, align_bytes=64)
-            share = HALF // 2
-            dst = lambda c0: grouped[:, c0 : c0 + share, :].rearrange("p (c i) t -> p c t i", i=4)
-            src = lambda c0: q_raw[h][:, :, c0 : c0 + share].rearrange("p t (c i) -> p c t i", i=4)
-            nc.scalar.copy(out=dst(0), in_=src(0))
-            nc.vector.tensor_copy(out=dst(share), in_=src(share))
+            dst = lambda c0, c1: grouped[:, c0:c1, :].rearrange("p (c i) t -> p c t i", i=4)
+            src = lambda c0, c1: q_raw[h][:, :, c0:c1].rearrange("p t (c i) -> p c t i", i=4)
+            nc.scalar.copy(out=dst(0, share), in_=src(0, share))
+            if share < HALF:
+                nc.vector.tensor_copy(out=dst(share, HALF), in_=src(share, HALF))
             nc.vector.quantize_mx(
                 out=q_code[:, h * HALF : (h + 1) * HALF].bitcast(FP8X4),
                 scales=q_scale[:, h * HALF : (h + 1) * HALF],
                 in_=grouped[:].rearrange("p w t -> p (w t)"),
             )
 
-        quantize_half(0)
+        quantize_half(0, HALF)
 
         bias = keep.tile([P, TILES], F32, name="bias", align_bytes=64)
         nc.scalar.activation(out=bias[:], in_=bias_turned[:, :, BIAS_ROW], func=ACT.Copy, scale=1.0 / SEG)
 
-        k_scale = keep.tile([P, N], U8, name="k_scale", align_bytes=64)
-        nc.vector.tensor_copy(out=k_scale[:], in_=scale_pool[:].bitcast(U8).indirect(offsets[:]))
         k_code = keep.tile([P, N], U32, name="k_code", align_bytes=64)
         for h in range(2):
             nc.vector.tensor_copy(
@@ -92,7 +94,7 @@ def tile_attend_tok_meanact_topk_kernel(tc, qT, k_words, k_scales, nb, offs, out
                 in_=word_pool[:].bitcast(U32).indirect(offsets[:, h * 16 : (h + 1) * 16]),
             )
 
-        quantize_half(1)
+        quantize_half(1, HALF // 2)
 
         active = keep.tile([P, TILES, NQ], F32, name="active", tag="stage1", align_bytes=64)
         means = keep.tile([P, TILES, RUNS], F32, name="means", align_bytes=64)

@@ -35,11 +35,15 @@ def tile_attend_tok_meanact_topk_kernel(tc, qT, k_words, k_scales, nb, offs, out
         offsets = keep.tile([P, N // 16], U16, name="offsets")
         nc.sync.dma_start(offsets[:], offs)
 
+        one = keep.tile([P, 1], F32, name="one", align_bytes=64)
+        nc.vector.memset(one[:], 1.0)
         scale_pool = keep.tile([P, T // 4], I32, name="scale_pool", tag="scales_then_codes", align_bytes=64)
         nc.vector.memset(scale_pool[:], 0)
-        bias_pool = keep.tile([P, T], F32, name="bias_pool", align_bytes=64)
+        bias_pool = keep.tile([P, T], F32, name="bias_pool", tag="bias_then_picked", align_bytes=64)
         nc.vector.memset(bias_pool[0:BIAS_ROW, :], 0.0)
-        nc.sync.dma_start(out=bias_pool[BIAS_ROW:P, :], in_=nb[0:1, :])
+        nc.scalar.dma_start(out=bias_pool[BIAS_ROW:P, :], in_=nb[0:1, :])
+        mean_factor = keep.tile([P, 1], F32, name="mean_factor", align_bytes=64)
+        nc.scalar.activation(out=mean_factor[:], in_=one[:], func=ACT.Copy, scale=1.0 / SEG)
 
         q_rows = qT[0].rearrange("(p j) w -> p j w", j=PACK)
         q_raw = [keep.tile([P, PACK, HALF], F32, name="q_raw%d" % h, tag="stage%d" % h, align_bytes=64) for h in range(2)]
@@ -60,7 +64,7 @@ def tile_attend_tok_meanact_topk_kernel(tc, qT, k_words, k_scales, nb, offs, out
         for m in range(TILES):
             nc.tensor.transpose(bias_turned[:, m, :], bias_rows[:, m * P : (m + 1) * P], ident[:])
 
-        scale_picked = keep.tile([P, N], U8, name="scale_picked", align_bytes=64)
+        scale_picked = keep.tile([P, N], U8, name="scale_picked", tag="bias_then_picked", align_bytes=64)
         nc.vector.tensor_copy(out=scale_picked[:], in_=scale_pool[:].bitcast(U8).indirect(offsets[:]))
         for r in range(4):
             nc.sync.dma_start(out=k_scale_words[r:P:32, :], in_=scale_picked[8 * r : P : 32, :].bitcast(I32))
@@ -85,7 +89,7 @@ def tile_attend_tok_meanact_topk_kernel(tc, qT, k_words, k_scales, nb, offs, out
         quantize_half(0, HALF)
 
         bias = keep.tile([P, TILES], F32, name="bias", align_bytes=64)
-        nc.scalar.activation(out=bias[:], in_=bias_turned[:, :, BIAS_ROW], func=ACT.Copy, scale=1.0 / SEG)
+        nc.scalar.activation(out=bias[:], in_=bias_turned[:, :, BIAS_ROW], func=ACT.Copy, scale=mean_factor[:])
 
         k_code = keep.tile([P, N], U32, name="k_code", align_bytes=64)
         for h in range(2):

@@ -23,7 +23,7 @@ AX = mybir.AxisListType
 
 BIAS_ROW = P - 1
 HALF = NQ // 2
-PIECES = [(m, c0, 256) for c0 in (0, 256) for m in range(TILES)]
+PIECES = [(0, 0, 128), (0, 128, 128)] + [(m, c0, 256) for c0 in (0, 256) for m in range(TILES)][1:]
 
 
 def tile_attend_tok_meanact_topk_kernel(tc, qT, k_words, k_scales, nb, offs, out):
@@ -37,7 +37,7 @@ def tile_attend_tok_meanact_topk_kernel(tc, qT, k_words, k_scales, nb, offs, out
 
         one = keep.tile([P, 1], F32, name="one", align_bytes=64)
         nc.vector.memset(one[:], 1.0)
-        scale_pool = keep.tile([P, T // 4], I32, name="scale_pool", tag="scales_then_codes", align_bytes=64)
+        scale_pool = keep.tile([P, T // 4], I32, name="scale_pool", align_bytes=64)
         nc.vector.memset(scale_pool[:], 0)
         bias_pool = keep.tile([P, T], F32, name="bias_pool", tag="bias_then_picked", align_bytes=64)
         nc.vector.memset(bias_pool[0:BIAS_ROW, :], 0.0)
@@ -50,7 +50,6 @@ def tile_attend_tok_meanact_topk_kernel(tc, qT, k_words, k_scales, nb, offs, out
         nc.sync.dma_start(out=q_raw[0][:], in_=q_rows[:, :, 0:HALF])
         nc.sync.dma_start(out=scale_pool[0:P:8, :], in_=k_scales[0].bitcast(I32))
         k_scale_words = keep.tile([P, N // 4], I32, name="k_scale_words", align_bytes=64)
-        nc.vector.memset(k_scale_words[:], 0)
         word_pool = keep.tile([P, T], I32, name="word_pool", align_bytes=64)
         nc.sync.dma_start(out=word_pool[:], in_=k_words[0].rearrange("p n t -> p (n t)").bitcast(I32))
         nc.sync.dma_start(out=q_raw[1][:], in_=q_rows[:, :, HALF:NQ])
@@ -70,7 +69,7 @@ def tile_attend_tok_meanact_topk_kernel(tc, qT, k_words, k_scales, nb, offs, out
             nc.sync.dma_start(out=k_scale_words[r:P:32, :], in_=scale_picked[8 * r : P : 32, :].bitcast(I32))
         k_scale = k_scale_words[:].bitcast(U8)
 
-        q_code = keep.tile([P, NQ], U32, name="q_code", tag="scales_then_codes", align_bytes=64)
+        q_code = keep.tile([P, NQ], U32, name="q_code", align_bytes=64)
         q_scale = keep.tile([P, NQ], U8, name="q_scale", align_bytes=64)
 
         def quantize_half(h, share):
@@ -98,13 +97,13 @@ def tile_attend_tok_meanact_topk_kernel(tc, qT, k_words, k_scales, nb, offs, out
                 in_=word_pool[:].bitcast(U32).indirect(offsets[:, h * 16 : (h + 1) * 16]),
             )
 
-        quantize_half(1, HALF // 2)
+        quantize_half(1, 112)
 
-        active = keep.tile([P, TILES, NQ], F32, name="active", tag="stage1", align_bytes=64)
+        active = keep.tile([P, TILES, NQ], F32, name="active", align_bytes=64)
         means = keep.tile([P, TILES, RUNS], F32, name="means", align_bytes=64)
         out_view = out[0].rearrange("(m p) j -> p m j", p=P)
         for index, (m, c0, width) in enumerate(PIECES):
-            acc = psum.tile([P, width], F32, name="acc%d" % index, tag="bank%d" % index)
+            acc = psum.tile([P, width], F32, name="acc%d" % index, tag="bank%d" % (index % 8))
             nc.tensor.matmul_mx(
                 out=acc[:],
                 lhsT=k_code[:, m * P : (m + 1) * P].bitcast(FP8X4),
@@ -114,14 +113,29 @@ def tile_attend_tok_meanact_topk_kernel(tc, qT, k_words, k_scales, nb, offs, out
                 start=True,
                 stop=True,
             )
+            plain = width - 3 * SEG if index == len(PIECES) - 1 else width
             nc.scalar.activation(
-                out=active[:, m, c0 : c0 + width], in_=acc[:], func=ACT.Relu, bias=bias[:, m : m + 1], scale=1.0 / SEG
+                out=active[:, m, c0 : c0 + plain],
+                in_=acc[:, 0:plain],
+                func=ACT.Relu,
+                bias=bias[:, m : m + 1],
+                scale=1.0 / SEG,
             )
             nc.vector.tensor_reduce(
-                out=means[:, m, c0 // SEG : (c0 + width) // SEG],
-                in_=active[:, m, c0 : c0 + width].rearrange("p (j e) -> p j e", e=SEG),
+                out=means[:, m, c0 // SEG : (c0 + plain) // SEG],
+                in_=active[:, m, c0 : c0 + plain].rearrange("p (j e) -> p j e", e=SEG),
                 axis=AX.X,
                 op=ALU.add,
             )
+            for c in range(plain, width, SEG):
+                j = (c0 + c) // SEG
+                nc.scalar.activation(
+                    out=active[:, m, c0 + c : c0 + c + SEG],
+                    in_=acc[:, c : c + SEG],
+                    func=ACT.Relu,
+                    bias=bias[:, m : m + 1],
+                    scale=1.0 / SEG,
+                    accum_out=means[:, m, j : j + 1],
+                )
             if c0 + width == NQ:
                 nc.sync.dma_start(out=out_view[:, m, :], in_=means[:, m, :])

@@ -35,45 +35,45 @@ def tile_attend_tok_meanact_topk_kernel(tc, qT, k_words, k_scales, nb, offs, out
         offsets = keep.tile([P, N // 16], U16, name="offsets")
         nc.sync.dma_start(offsets[:], offs)
 
-        one = keep.tile([P, 1], F32, name="one", align_bytes=64)
+        one = keep.tile([P, 1], F32, name="one", align_bytes=256)
         nc.vector.memset(one[:], 1.0)
-        scale_pool = keep.tile([P, T // 4], I32, name="scale_pool", align_bytes=64)
+        scale_pool = keep.tile([P, T // 4], I32, name="scale_pool", align_bytes=256)
         nc.vector.memset(scale_pool[:], 0)
-        bias_pool = keep.tile([P, T], F32, name="bias_pool", tag="bias_then_picked", align_bytes=64)
+        bias_pool = keep.tile([P, T], F32, name="bias_pool", tag="bias_then_picked", align_bytes=256)
         nc.vector.memset(bias_pool[0:BIAS_ROW, :], 0.0)
         nc.scalar.dma_start(out=bias_pool[BIAS_ROW:P, :], in_=nb[0:1, :])
-        mean_factor = keep.tile([P, 1], F32, name="mean_factor", align_bytes=64)
+        mean_factor = keep.tile([P, 1], F32, name="mean_factor", align_bytes=256)
         nc.scalar.activation(out=mean_factor[:], in_=one[:], func=ACT.Copy, scale=1.0 / SEG)
 
         q_rows = qT[0].rearrange("(p j) w -> p j w", j=PACK)
-        q_raw = [keep.tile([P, PACK, HALF], F32, name="q_raw%d" % h, tag="stage%d" % h, align_bytes=64) for h in range(2)]
+        q_raw = [keep.tile([P, PACK, HALF], F32, name="q_raw%d" % h, tag="stage%d" % h, align_bytes=256) for h in range(2)]
         nc.sync.dma_start(out=q_raw[0][:], in_=q_rows[:, :, 0:HALF])
         nc.sync.dma_start(out=scale_pool[0:P:8, :], in_=k_scales[0].bitcast(I32))
-        k_scale_words = keep.tile([P, N // 4], I32, name="k_scale_words", align_bytes=64)
-        word_pool = keep.tile([P, T], I32, name="word_pool", align_bytes=64)
+        k_scale_words = keep.tile([P, N // 4], I32, name="k_scale_words", align_bytes=256)
+        word_pool = keep.tile([P, T], I32, name="word_pool", align_bytes=256)
         nc.sync.dma_start(out=word_pool[:], in_=k_words[0].rearrange("p n t -> p (n t)").bitcast(I32))
         nc.sync.dma_start(out=q_raw[1][:], in_=q_rows[:, :, HALF:NQ])
 
-        ident = keep.tile([P, P], F32, name="ident", align_bytes=64)
+        ident = keep.tile([P, P], F32, name="ident", align_bytes=256)
         make_identity(nc, ident[:])
 
-        bias_rows = keep.tile([P, N], F32, name="bias_rows", align_bytes=64)
+        bias_rows = keep.tile([P, N], F32, name="bias_rows", align_bytes=256)
         nc.vector.tensor_copy(out=bias_rows[:], in_=bias_pool[:].indirect(offsets[:]))
         bias_turned = psum.tile([P, TILES, P], F32, name="bias_turned", tag="bank7")
         for m in range(TILES):
             nc.tensor.transpose(bias_turned[:, m, :], bias_rows[:, m * P : (m + 1) * P], ident[:])
 
-        scale_picked = keep.tile([P, N], U8, name="scale_picked", tag="bias_then_picked", align_bytes=64)
+        scale_picked = keep.tile([P, N], U8, name="scale_picked", tag="bias_then_picked", align_bytes=256)
         nc.vector.tensor_copy(out=scale_picked[:], in_=scale_pool[:].bitcast(U8).indirect(offsets[:]))
         for r in range(4):
             nc.sync.dma_start(out=k_scale_words[r:P:32, :], in_=scale_picked[8 * r : P : 32, :].bitcast(I32))
         k_scale = k_scale_words[:].bitcast(U8)
 
-        q_code = keep.tile([P, NQ], U32, name="q_code", align_bytes=64)
-        q_scale = keep.tile([P, NQ], U8, name="q_scale", align_bytes=64)
+        q_code = keep.tile([P, NQ], U32, name="q_code", align_bytes=256)
+        q_scale = keep.tile([P, NQ], U8, name="q_scale", align_bytes=256)
 
         def quantize_half(h, share):
-            grouped = keep.tile([P, HALF, PACK], BF16, name="q_grouped%d" % h, align_bytes=64)
+            grouped = keep.tile([P, HALF, PACK], BF16, name="q_grouped%d" % h, align_bytes=256)
             dst = lambda c0, c1: grouped[:, c0:c1, :].rearrange("p (c i) t -> p c t i", i=4)
             src = lambda c0, c1: q_raw[h][:, :, c0:c1].rearrange("p t (c i) -> p c t i", i=4)
             nc.scalar.copy(out=dst(0, share), in_=src(0, share))
@@ -87,10 +87,10 @@ def tile_attend_tok_meanact_topk_kernel(tc, qT, k_words, k_scales, nb, offs, out
 
         quantize_half(0, HALF)
 
-        bias = keep.tile([P, TILES], F32, name="bias", align_bytes=64)
+        bias = keep.tile([P, TILES], F32, name="bias", align_bytes=256)
         nc.scalar.activation(out=bias[:], in_=bias_turned[:, :, BIAS_ROW], func=ACT.Copy, scale=mean_factor[:])
 
-        k_code = keep.tile([P, N], U32, name="k_code", align_bytes=64)
+        k_code = keep.tile([P, N], U32, name="k_code", align_bytes=256)
         for h in range(2):
             nc.vector.tensor_copy(
                 out=k_code[:, h * 256 : (h + 1) * 256],
@@ -99,8 +99,8 @@ def tile_attend_tok_meanact_topk_kernel(tc, qT, k_words, k_scales, nb, offs, out
 
         quantize_half(1, 112)
 
-        active = keep.tile([P, TILES, NQ], F32, name="active", align_bytes=64)
-        means = keep.tile([P, TILES, RUNS], F32, name="means", align_bytes=64)
+        active = keep.tile([P, TILES, NQ], F32, name="active", align_bytes=256)
+        means = keep.tile([P, TILES, RUNS], F32, name="means", align_bytes=256)
         out_view = out[0].rearrange("(m p) j -> p m j", p=P)
         for index, (m, c0, width) in enumerate(PIECES):
             acc = psum.tile([P, width], F32, name="acc%d" % index, tag="bank%d" % (index % 8))

@@ -48,7 +48,7 @@ def tile_attend_tok_meanact_topk_kernel(tc, qT, k_words, k_scales, nb, offs, out
         q_rows = qT[0].rearrange("(p j) w -> p j w", j=PACK)
         q_raw = [keep.tile([P, PACK, HALF], F32, name="q_raw%d" % h, tag="stage%d" % h, align_bytes=256) for h in range(2)]
         nc.sync.dma_start(out=q_raw[0][:], in_=q_rows[:, :, 0:HALF])
-        nc.sync.dma_start(out=scale_pool[0:P:8, :], in_=k_scales[0].bitcast(I32))
+        nc.sync.dma_start(out=scale_pool[32:96:4, :], in_=k_scales[0].bitcast(I32))
         k_scale_words = keep.tile([P, N // 4], I32, name="k_scale_words", align_bytes=256)
         word_pool = keep.tile([P, T], I32, name="word_pool", align_bytes=256)
         nc.sync.dma_start(out=word_pool[:], in_=k_words[0].rearrange("p n t -> p (n t)").bitcast(I32))
@@ -66,7 +66,7 @@ def tile_attend_tok_meanact_topk_kernel(tc, qT, k_words, k_scales, nb, offs, out
         scale_picked = keep.tile([P, N], U8, name="scale_picked", tag="bias_then_picked", align_bytes=256)
         nc.vector.tensor_copy(out=scale_picked[:], in_=scale_pool[:].bitcast(U8).indirect(offsets[:]))
         for r in range(4):
-            nc.sync.dma_start(out=k_scale_words[r:P:32, :], in_=scale_picked[8 * r : P : 32, :].bitcast(I32))
+            nc.sync.dma_start(out=k_scale_words[r:P:32, :], in_=scale_picked[32 + 4 * r : 96 : 16, :].bitcast(I32))
         k_scale = k_scale_words[:].bitcast(U8)
 
         q_code = keep.tile([P, NQ], U32, name="q_code", align_bytes=256)

@@ -23,7 +23,7 @@ AX = mybir.AxisListType
 
 BIAS_ROW = P - 1
 HALF = NQ // 2
-PIECES = [(0, 0, 128), (0, 128, 128)] + [(m, c0, 256) for c0 in (0, 256) for m in range(TILES)][1:]
+QUARTER = NQ // 4
 
 
 def tile_attend_tok_meanact_topk_kernel(tc, qT, k_words, k_scales, nb, offs, out):
@@ -35,24 +35,24 @@ def tile_attend_tok_meanact_topk_kernel(tc, qT, k_words, k_scales, nb, offs, out
         offsets = keep.tile([P, N // 16], U16, name="offsets")
         nc.sync.dma_start(offsets[:], offs)
 
-        one = keep.tile([P, 1], F32, name="one", align_bytes=256)
-        nc.vector.memset(one[:], 1.0)
-        scale_pool = keep.tile([P, T // 4], I32, name="scale_pool", align_bytes=256)
+        scale_pool = keep.tile([P, T // 4], I32, name="scale_pool", tag="scales_then_last_q", align_bytes=256)
         nc.vector.memset(scale_pool[:], 0)
         bias_pool = keep.tile([P, T], F32, name="bias_pool", tag="bias_then_picked", align_bytes=256)
         nc.vector.memset(bias_pool[0:BIAS_ROW, :], 0.0)
         nc.scalar.dma_start(out=bias_pool[BIAS_ROW:P, :], in_=nb[0:1, :])
+        one = keep.tile([P, 1], F32, name="one", align_bytes=256)
+        nc.gpsimd.memset(one[:], 1.0)
         mean_factor = keep.tile([P, 1], F32, name="mean_factor", align_bytes=256)
         nc.scalar.activation(out=mean_factor[:], in_=one[:], func=ACT.Copy, scale=1.0 / SEG)
 
         q_rows = qT[0].rearrange("(p j) w -> p j w", j=PACK)
-        q_raw = [keep.tile([P, PACK, HALF], F32, name="q_raw%d" % h, tag="stage%d" % h, align_bytes=256) for h in range(2)]
-        nc.sync.dma_start(out=q_raw[0][:], in_=q_rows[:, :, 0:HALF])
+        q_half = keep.tile([P, PACK, HALF], F32, name="q_half", align_bytes=256)
+        nc.sync.dma_start(out=q_half[:], in_=q_rows[:, :, 0:HALF])
         nc.sync.dma_start(out=scale_pool[32:96:4, :], in_=k_scales[0].bitcast(I32))
-        k_scale_words = keep.tile([P, N // 4], I32, name="k_scale_words", align_bytes=256)
-        word_pool = keep.tile([P, T], I32, name="word_pool", align_bytes=256)
+        word_pool = keep.tile([P, T], I32, name="word_pool", tag="words_then_plane", align_bytes=256)
         nc.sync.dma_start(out=word_pool[:], in_=k_words[0].rearrange("p n t -> p (n t)").bitcast(I32))
-        nc.sync.dma_start(out=q_raw[1][:], in_=q_rows[:, :, HALF:NQ])
+        q_third = keep.tile([P, PACK, QUARTER], F32, name="q_third", align_bytes=256)
+        nc.sync.dma_start(out=q_third[:], in_=q_rows[:, :, HALF : HALF + QUARTER])
 
         ident = keep.tile([P, P], F32, name="ident", align_bytes=256)
         make_identity(nc, ident[:])
@@ -65,27 +65,25 @@ def tile_attend_tok_meanact_topk_kernel(tc, qT, k_words, k_scales, nb, offs, out
 
         scale_picked = keep.tile([P, N], U8, name="scale_picked", tag="bias_then_picked", align_bytes=256)
         nc.vector.tensor_copy(out=scale_picked[:], in_=scale_pool[:].bitcast(U8).indirect(offsets[:]))
+        k_scale_words = keep.tile([P, N // 4], I32, name="k_scale_words", align_bytes=256)
         for r in range(4):
             nc.sync.dma_start(out=k_scale_words[r:P:32, :], in_=scale_picked[32 + 4 * r : 96 : 16, :].bitcast(I32))
         k_scale = k_scale_words[:].bitcast(U8)
+        q_last = keep.tile([P, PACK, QUARTER], F32, name="q_last", tag="scales_then_last_q", align_bytes=256)
+        nc.sync.dma_start(out=q_last[:], in_=q_rows[:, :, HALF + QUARTER : NQ])
 
-        q_code = keep.tile([P, NQ], U32, name="q_code", align_bytes=256)
-        q_scale = keep.tile([P, NQ], U8, name="q_scale", align_bytes=256)
-
-        def quantize_half(h, share):
-            grouped = keep.tile([P, HALF, PACK], BF16, name="q_grouped%d" % h, align_bytes=256)
-            dst = lambda c0, c1: grouped[:, c0:c1, :].rearrange("p (c i) t -> p c t i", i=4)
-            src = lambda c0, c1: q_raw[h][:, :, c0:c1].rearrange("p t (c i) -> p c t i", i=4)
-            nc.scalar.copy(out=dst(0, share), in_=src(0, share))
-            if share < HALF:
-                nc.vector.tensor_copy(out=dst(share, HALF), in_=src(share, HALF))
-            nc.vector.quantize_mx(
-                out=q_code[:, h * HALF : (h + 1) * HALF].bitcast(FP8X4),
-                scales=q_scale[:, h * HALF : (h + 1) * HALF],
-                in_=grouped[:].rearrange("p w t -> p (w t)"),
+        def quantize(name, raw, width, cast, plane_tag):
+            grouped = keep.tile([P, width, PACK], BF16, name="grouped_" + name, align_bytes=256)
+            cast(
+                out=grouped[:].rearrange("p (c i) t -> p c t i", i=4),
+                in_=raw[:].rearrange("p t (c i) -> p c t i", i=4),
             )
+            code = keep.tile([P, width], U32, name="code_" + name, align_bytes=256)
+            plane = keep.tile([P, width], U8, name="plane_" + name, tag=plane_tag, align_bytes=256)
+            nc.vector.quantize_mx(out=code[:].bitcast(FP8X4), scales=plane[:], in_=grouped[:].rearrange("p w t -> p (w t)"))
+            return code, plane
 
-        quantize_half(0, HALF)
+        half = quantize("half", q_half, HALF, nc.scalar.copy, "plane_half")
 
         bias = keep.tile([P, TILES], F32, name="bias", align_bytes=256)
         nc.scalar.activation(out=bias[:], in_=bias_turned[:, :, BIAS_ROW], func=ACT.Copy, scale=mean_factor[:])
@@ -97,45 +95,46 @@ def tile_attend_tok_meanact_topk_kernel(tc, qT, k_words, k_scales, nb, offs, out
                 in_=word_pool[:].bitcast(U32).indirect(offsets[:, h * 16 : (h + 1) * 16]),
             )
 
-        quantize_half(1, 112)
+        third = quantize("third", q_third, QUARTER, nc.scalar.copy, "words_then_plane")
+        last = quantize("last", q_last, QUARTER, nc.vector.tensor_copy, "plane_last")
 
-        active = keep.tile([P, TILES, NQ], F32, name="active", align_bytes=256)
+        active = keep.tile([P, TILES, RUNS, SEG], F32, name="active", align_bytes=256)
         means = keep.tile([P, TILES, RUNS], F32, name="means", align_bytes=256)
         out_view = out[0].rearrange("(m p) j -> p m j", p=P)
-        for index, (m, c0, width) in enumerate(PIECES):
-            acc = psum.tile([P, width], F32, name="acc%d" % index, tag="bank%d" % (index % 8))
-            nc.tensor.matmul_mx(
-                out=acc[:],
-                lhsT=k_code[:, m * P : (m + 1) * P].bitcast(FP8X4),
-                lhsT_scale=k_scale[:, m * P : (m + 1) * P],
-                rhs=q_code[:, c0 : c0 + width].bitcast(FP8X4),
-                rhs_scale=q_scale[:, c0 : c0 + width],
-                start=True,
-                stop=True,
-            )
-            plain = width - 3 * SEG if index == len(PIECES) - 1 else width
-            nc.scalar.activation(
-                out=active[:, m, c0 : c0 + plain],
-                in_=acc[:, 0:plain],
-                func=ACT.Relu,
-                bias=bias[:, m : m + 1],
-                scale=1.0 / SEG,
-            )
-            nc.vector.tensor_reduce(
-                out=means[:, m, c0 // SEG : (c0 + plain) // SEG],
-                in_=active[:, m, c0 : c0 + plain].rearrange("p (j e) -> p j e", e=SEG),
-                axis=AX.X,
-                op=ALU.add,
-            )
-            for c in range(plain, width, SEG):
-                j = (c0 + c) // SEG
-                nc.scalar.activation(
-                    out=active[:, m, c0 + c : c0 + c + SEG],
-                    in_=acc[:, c : c + SEG],
-                    func=ACT.Relu,
-                    bias=bias[:, m : m + 1],
-                    scale=1.0 / SEG,
-                    accum_out=means[:, m, j : j + 1],
+
+        def add_up(tiles, runs):
+            nc.vector.tensor_reduce(out=means[:, tiles, runs], in_=active[:, tiles, runs, :], axis=AX.X, op=ALU.add)
+
+        parts = ((half, 0, 8, {0: 0, 2: 1, 3: 3}), (third, 8, 12, {3: 0}), (last, 12, 16, {2: 0}))
+        index = 0
+        for (code, plane), j0, j1, sums_from in parts:
+            for m in range(TILES):
+                acc = psum.tile([P, j1 - j0, SEG], F32, name="acc%d" % index, tag="bank%d" % (index % 8))
+                index = index + 1
+                nc.tensor.matmul_mx(
+                    out=acc[:].rearrange("p j e -> p (j e)"),
+                    lhsT=k_code[:, m * P : (m + 1) * P].bitcast(FP8X4),
+                    lhsT_scale=k_scale[:, m * P : (m + 1) * P],
+                    rhs=code[:].bitcast(FP8X4),
+                    rhs_scale=plane[:],
+                    start=True,
+                    stop=True,
                 )
-            if c0 + width == NQ:
-                nc.sync.dma_start(out=out_view[:, m, :], in_=means[:, m, :])
+                if j1 == RUNS and m == TILES - 1:
+                    for j in range(j0, j1):
+                        nc.scalar.activation(
+                            out=active[:, m, j, :],
+                            in_=acc[:, j - j0, :],
+                            func=ACT.Relu,
+                            bias=bias[:, m : m + 1],
+                            scale=1.0 / SEG,
+                            accum_out=means[:, m, j : j + 1],
+                        )
+                else:
+                    nc.scalar.activation(
+                        out=active[:, m, j0:j1, :], in_=acc[:], func=ACT.Relu, bias=bias[:, m : m + 1], scale=1.0 / SEG
+                    )
+                if m in sums_from:
+                    add_up(slice(sums_from[m], m + 1), slice(j0, j1))
+        nc.sync.dma_start(out=out_view[:, TILES - 1 : TILES, :], in_=means[:, TILES - 1 : TILES, :])
+        nc.sync.dma_start(out=out_view[:, 0 : TILES - 1, :], in_=means[:, 0 : TILES - 1, :])

@@ -37,7 +37,7 @@ def tile_attend_tok_meanact_topk_kernel(tc, qT, k_words, k_scales, nb, offs, out
 
         scale_pool = keep.tile([P, T // 4], I32, name="scale_pool", tag="scales_then_last_q", align_bytes=256)
         nc.vector.memset(scale_pool[:], 0)
-        bias_pool = keep.tile([P, T], F32, name="bias_pool", tag="bias_then_picked", align_bytes=256)
+        bias_pool = keep.tile([P, T], F32, name="bias_pool", tag="bias_then_grouped", align_bytes=256)
         nc.vector.memset(bias_pool[0:BIAS_ROW, :], 0.0)
         nc.scalar.dma_start(out=bias_pool[BIAS_ROW:P, :], in_=nb[0:1, :])
         one = keep.tile([P, 1], F32, name="one", align_bytes=256)
@@ -47,8 +47,9 @@ def tile_attend_tok_meanact_topk_kernel(tc, qT, k_words, k_scales, nb, offs, out
 
         q_rows = qT[0].rearrange("(p j) w -> p j w", j=PACK)
         q_half = keep.tile([P, PACK, HALF], F32, name="q_half", align_bytes=256)
-        nc.sync.dma_start(out=q_half[:], in_=q_rows[:, :, 0:HALF])
+        nc.sync.dma_start(out=q_half[:, 0:2, :], in_=q_rows[:, 0:2, 0:HALF])
         nc.sync.dma_start(out=scale_pool[32:96:4, :], in_=k_scales[0].bitcast(I32))
+        nc.sync.dma_start(out=q_half[:, 2:4, :], in_=q_rows[:, 2:4, 0:HALF])
         word_pool = keep.tile([P, T], I32, name="word_pool", tag="words_then_plane", align_bytes=256)
         nc.sync.dma_start(out=word_pool[:], in_=k_words[0].rearrange("p n t -> p (n t)").bitcast(I32))
         q_third = keep.tile([P, PACK, QUARTER], F32, name="q_third", align_bytes=256)
@@ -58,12 +59,12 @@ def tile_attend_tok_meanact_topk_kernel(tc, qT, k_words, k_scales, nb, offs, out
         make_identity(nc, ident[:])
 
         bias_rows = keep.tile([P, N], F32, name="bias_rows", align_bytes=256)
-        nc.vector.tensor_copy(out=bias_rows[:], in_=bias_pool[:].indirect(offsets[:]))
+        nc.scalar.activation(out=bias_rows[:], in_=bias_pool[:].indirect(offsets[:]), func=ACT.Copy)
         bias_turned = psum.tile([P, TILES, P], F32, name="bias_turned", tag="bank7")
         for m in range(TILES):
             nc.tensor.transpose(bias_turned[:, m, :], bias_rows[:, m * P : (m + 1) * P], ident[:])
 
-        scale_picked = keep.tile([P, N], U8, name="scale_picked", tag="bias_then_picked", align_bytes=256)
+        scale_picked = keep.tile([P, N], U8, name="scale_picked", align_bytes=256)
         nc.vector.tensor_copy(out=scale_picked[:], in_=scale_pool[:].bitcast(U8).indirect(offsets[:]))
         k_scale_words = keep.tile([P, N // 4], I32, name="k_scale_words", align_bytes=256)
         for r in range(4):
@@ -72,18 +73,20 @@ def tile_attend_tok_meanact_topk_kernel(tc, qT, k_words, k_scales, nb, offs, out
         q_last = keep.tile([P, PACK, QUARTER], F32, name="q_last", tag="scales_then_last_q", align_bytes=256)
         nc.sync.dma_start(out=q_last[:], in_=q_rows[:, :, HALF + QUARTER : NQ])
 
-        def quantize(name, raw, width, cast, plane_tag):
-            grouped = keep.tile([P, width, PACK], BF16, name="grouped_" + name, align_bytes=256)
-            cast(
-                out=grouped[:].rearrange("p (c i) t -> p c t i", i=4),
-                in_=raw[:].rearrange("p t (c i) -> p c t i", i=4),
-            )
+        def quantize(name, raw, width, share, grouped_tag, plane_tag):
+            grouped = keep.tile([P, width, PACK], BF16, name="grouped_" + name, tag=grouped_tag, align_bytes=256)
+            dst = lambda c0, c1: grouped[:, c0:c1, :].rearrange("p (c i) t -> p c t i", i=4)
+            src = lambda c0, c1: raw[:, :, c0:c1].rearrange("p t (c i) -> p c t i", i=4)
+            if share > 0:
+                nc.scalar.copy(out=dst(0, share), in_=src(0, share))
+            if share < width:
+                nc.vector.tensor_copy(out=dst(share, width), in_=src(share, width))
             code = keep.tile([P, width], U32, name="code_" + name, align_bytes=256)
             plane = keep.tile([P, width], U8, name="plane_" + name, tag=plane_tag, align_bytes=256)
             nc.vector.quantize_mx(out=code[:].bitcast(FP8X4), scales=plane[:], in_=grouped[:].rearrange("p w t -> p (w t)"))
             return code, plane
 
-        half = quantize("half", q_half, HALF, nc.scalar.copy, "plane_half")
+        half = quantize("half", q_half, HALF, HALF // 2, "bias_then_grouped", "plane_half")
 
         bias = keep.tile([P, TILES], F32, name="bias", align_bytes=256)
         nc.scalar.activation(out=bias[:], in_=bias_turned[:, :, BIAS_ROW], func=ACT.Copy, scale=mean_factor[:])
@@ -95,46 +98,69 @@ def tile_attend_tok_meanact_topk_kernel(tc, qT, k_words, k_scales, nb, offs, out
                 in_=word_pool[:].bitcast(U32).indirect(offsets[:, h * 16 : (h + 1) * 16]),
             )
 
-        third = quantize("third", q_third, QUARTER, nc.scalar.copy, "words_then_plane")
-        last = quantize("last", q_last, QUARTER, nc.vector.tensor_copy, "plane_last")
+        third = quantize("third", q_third, QUARTER, QUARTER, "grouped_third", "words_then_plane")
+        last = quantize("last", q_last, QUARTER, 0, "grouped_last", "plane_last")
 
         active = keep.tile([P, TILES, RUNS, SEG], F32, name="active", align_bytes=256)
         means = keep.tile([P, TILES, RUNS], F32, name="means", align_bytes=256)
         out_view = out[0].rearrange("(m p) j -> p m j", p=P)
 
-        def add_up(tiles, runs):
-            nc.vector.tensor_reduce(out=means[:, tiles, runs], in_=active[:, tiles, runs, :], axis=AX.X, op=ALU.add)
-
-        parts = ((half, 0, 8, {0: 0, 2: 1, 3: 3}), (third, 8, 12, {3: 0}), (last, 12, 16, {2: 0}))
-        index = 0
-        for (code, plane), j0, j1, sums_from in parts:
-            for m in range(TILES):
-                acc = psum.tile([P, j1 - j0, SEG], F32, name="acc%d" % index, tag="bank%d" % (index % 8))
-                index = index + 1
-                nc.tensor.matmul_mx(
-                    out=acc[:].rearrange("p j e -> p (j e)"),
-                    lhsT=k_code[:, m * P : (m + 1) * P].bitcast(FP8X4),
-                    lhsT_scale=k_scale[:, m * P : (m + 1) * P],
-                    rhs=code[:].bitcast(FP8X4),
-                    rhs_scale=plane[:],
-                    start=True,
-                    stop=True,
+        def product(index, part, first_run, m, j0, j1, accumulated=0):
+            code, plane = part
+            cols = slice((j0 - first_run) * SEG, (j1 - first_run) * SEG)
+            acc = psum.tile([P, j1 - j0, SEG], F32, name="acc%d" % index, tag="bank%d" % (index % 8))
+            nc.tensor.matmul_mx(
+                out=acc[:].rearrange("p j e -> p (j e)"),
+                lhsT=k_code[:, m * P : (m + 1) * P].bitcast(FP8X4),
+                lhsT_scale=k_scale[:, m * P : (m + 1) * P],
+                rhs=code[:, cols].bitcast(FP8X4),
+                rhs_scale=plane[:, cols],
+                start=True,
+                stop=True,
+            )
+            plain = j1 - accumulated
+            if plain > j0:
+                nc.scalar.activation(
+                    out=active[:, m, j0:plain, :],
+                    in_=acc[:, 0 : plain - j0, :],
+                    func=ACT.Relu,
+                    bias=bias[:, m : m + 1],
+                    scale=1.0 / SEG,
                 )
-                if j1 == RUNS and m == TILES - 1:
-                    for j in range(j0, j1):
-                        nc.scalar.activation(
-                            out=active[:, m, j, :],
-                            in_=acc[:, j - j0, :],
-                            func=ACT.Relu,
-                            bias=bias[:, m : m + 1],
-                            scale=1.0 / SEG,
-                            accum_out=means[:, m, j : j + 1],
-                        )
-                else:
-                    nc.scalar.activation(
-                        out=active[:, m, j0:j1, :], in_=acc[:], func=ACT.Relu, bias=bias[:, m : m + 1], scale=1.0 / SEG
-                    )
-                if m in sums_from:
-                    add_up(slice(sums_from[m], m + 1), slice(j0, j1))
-        nc.sync.dma_start(out=out_view[:, TILES - 1 : TILES, :], in_=means[:, TILES - 1 : TILES, :])
-        nc.sync.dma_start(out=out_view[:, 0 : TILES - 1, :], in_=means[:, 0 : TILES - 1, :])
+            for j in range(plain, j1):
+                nc.scalar.activation(
+                    out=active[:, m, j, :],
+                    in_=acc[:, j - j0, :],
+                    func=ACT.Relu,
+                    bias=bias[:, m : m + 1],
+                    scale=1.0 / SEG,
+                    accum_out=means[:, m, j : j + 1],
+                )
+
+        def add_up(m0, m1, j0, j1):
+            nc.vector.tensor_reduce(out=means[:, m0:m1, j0:j1], in_=active[:, m0:m1, j0:j1, :], axis=AX.X, op=ALU.add)
+
+        def store(m0, m1):
+            nc.sync.dma_start(out=out_view[:, m0:m1, :], in_=means[:, m0:m1, :])
+
+        product(0, half, 0, 0, 0, 4)
+        product(1, half, 0, 0, 4, 8)
+        add_up(0, 1, 0, 8)
+        product(2, half, 0, 1, 0, 8)
+        product(3, half, 0, 2, 0, 8)
+        add_up(1, 3, 0, 8)
+        product(4, half, 0, 3, 0, 8)
+        product(5, third, 8, 3, 8, 12)
+        add_up(3, 4, 0, 12)
+        for m in range(3):
+            product(6 + m, third, 8, m, 8, 12)
+        add_up(0, 3, 8, 12)
+        for m in range(2):
+            product(9 + m, last, 12, m, 12, 16)
+        add_up(0, 2, 12, 16)
+        store(0, 2)
+        product(11, last, 12, 2, 12, 16)
+        add_up(2, 3, 12, 16)
+        product(12, last, 12, 3, 12, 16, accumulated=4)
+        store(2, 3)
+        store(3, 4)

@@ -36,9 +36,11 @@ def tile_attend_tok_meanact_topk_kernel(tc, qT, k_words, k_scales, nb, offs, out
         nc.sync.dma_start(offsets[:], offs)
 
         scale_pool = keep.tile([P, T // 4], I32, name="scale_pool", tag="scales_then_last_q", align_bytes=256)
-        nc.vector.memset(scale_pool[:], 0)
+        nc.vector.memset(scale_pool[0:48, :], 0)
+        nc.vector.memset(scale_pool[64:P, :], 0)
+        nc.sync.dma_start(out=scale_pool[48:64, :], in_=k_scales[0].bitcast(I32))
         bias_pool = keep.tile([P, T], F32, name="bias_pool", tag="bias_then_grouped", align_bytes=256)
-        nc.vector.memset(bias_pool[0:BIAS_ROW, :], 0.0)
+        nc.vector.memset(bias_pool[0:BIAS_ROW, 0 : T // 2], 0.0)
         nc.scalar.dma_start(out=bias_pool[BIAS_ROW:P, :], in_=nb[0:1, :])
         one = keep.tile([P, 1], F32, name="one", align_bytes=256)
         nc.gpsimd.memset(one[:], 1.0)
@@ -47,9 +49,7 @@ def tile_attend_tok_meanact_topk_kernel(tc, qT, k_words, k_scales, nb, offs, out
 
         q_rows = qT[0].rearrange("(p j) w -> p j w", j=PACK)
         q_half = keep.tile([P, PACK, HALF], F32, name="q_half", align_bytes=256)
-        nc.sync.dma_start(out=q_half[:, 0:2, :], in_=q_rows[:, 0:2, 0:HALF])
-        nc.sync.dma_start(out=scale_pool[32:96:4, :], in_=k_scales[0].bitcast(I32))
-        nc.sync.dma_start(out=q_half[:, 2:4, :], in_=q_rows[:, 2:4, 0:HALF])
+        nc.sync.dma_start(out=q_half[:], in_=q_rows[:, :, 0:HALF])
         word_pool = keep.tile([P, T], I32, name="word_pool", tag="words_then_plane", align_bytes=256)
         nc.sync.dma_start(out=word_pool[:], in_=k_words[0].rearrange("p n t -> p (n t)").bitcast(I32))
         q_third = keep.tile([P, PACK, QUARTER], F32, name="q_third", align_bytes=256)
@@ -57,6 +57,7 @@ def tile_attend_tok_meanact_topk_kernel(tc, qT, k_words, k_scales, nb, offs, out
 
         ident = keep.tile([P, P], F32, name="ident", align_bytes=256)
         make_identity(nc, ident[:])
+        nc.gpsimd.memset(bias_pool[0:BIAS_ROW, T // 2 : T], 0.0)
 
         bias_rows = keep.tile([P, N], F32, name="bias_rows", align_bytes=256)
         nc.scalar.activation(out=bias_rows[:], in_=bias_pool[:].indirect(offsets[:]), func=ACT.Copy)
@@ -68,7 +69,7 @@ def tile_attend_tok_meanact_topk_kernel(tc, qT, k_words, k_scales, nb, offs, out
         nc.vector.tensor_copy(out=scale_picked[:], in_=scale_pool[:].bitcast(U8).indirect(offsets[:]))
         k_scale_words = keep.tile([P, N // 4], I32, name="k_scale_words", align_bytes=256)
         for r in range(4):
-            nc.sync.dma_start(out=k_scale_words[r:P:32, :], in_=scale_picked[32 + 4 * r : 96 : 16, :].bitcast(I32))
+            nc.sync.dma_start(out=k_scale_words[r:P:32, :], in_=scale_picked[48 + r : 64 : 4, :].bitcast(I32))
         k_scale = k_scale_words[:].bitcast(U8)
         q_last = keep.tile([P, PACK, QUARTER], F32, name="q_last", tag="scales_then_last_q", align_bytes=256)
         nc.sync.dma_start(out=q_last[:], in_=q_rows[:, :, HALF + QUARTER : NQ])
@@ -86,7 +87,7 @@ def tile_attend_tok_meanact_topk_kernel(tc, qT, k_words, k_scales, nb, offs, out
             nc.vector.quantize_mx(out=code[:].bitcast(FP8X4), scales=plane[:], in_=grouped[:].rearrange("p w t -> p (w t)"))
             return code, plane
 
-        half = quantize("half", q_half, HALF, HALF // 2, "bias_then_grouped", "plane_half")
+        half = quantize("half", q_half, HALF, 0, "grouped_half", "plane_half")
 
         bias = keep.tile([P, TILES], F32, name="bias", align_bytes=256)
         nc.scalar.activation(out=bias[:], in_=bias_turned[:, :, BIAS_ROW], func=ACT.Copy, scale=mean_factor[:])
@@ -98,7 +99,7 @@ def tile_attend_tok_meanact_topk_kernel(tc, qT, k_words, k_scales, nb, offs, out
                 in_=word_pool[:].bitcast(U32).indirect(offsets[:, h * 16 : (h + 1) * 16]),
             )
 
-        third = quantize("third", q_third, QUARTER, QUARTER, "grouped_third", "words_then_plane")
+        third = quantize("third", q_third, QUARTER, QUARTER, "bias_then_grouped", "words_then_plane")
         last = quantize("last", q_last, QUARTER, 0, "grouped_last", "plane_last")
 
         active = keep.tile([P, TILES, RUNS, SEG], F32, name="active", align_bytes=256)

@@ -35,12 +35,12 @@ def tile_attend_tok_meanact_topk_kernel(tc, qT, k_words, k_scales, nb, offs, out
         offsets = keep.tile([P, N // 16], U16, name="offsets")
         nc.sync.dma_start(offsets[:], offs)
 
+        bias_pool = keep.tile([P, T], F32, name="bias_pool", tag="bias_then_grouped", align_bytes=256)
+        nc.vector.memset(bias_pool[0:BIAS_ROW, :], 0.0)
         scale_pool = keep.tile([P, T // 4], I32, name="scale_pool", tag="scales_then_last_q", align_bytes=256)
         nc.vector.memset(scale_pool[0:48, :], 0)
         nc.vector.memset(scale_pool[64:P, :], 0)
         nc.sync.dma_start(out=scale_pool[48:64, :], in_=k_scales[0].bitcast(I32))
-        bias_pool = keep.tile([P, T], F32, name="bias_pool", tag="bias_then_grouped", align_bytes=256)
-        nc.vector.memset(bias_pool[0:BIAS_ROW, 0 : T // 2], 0.0)
         nc.scalar.dma_start(out=bias_pool[BIAS_ROW:P, :], in_=nb[0:1, :])
         one = keep.tile([P, 1], F32, name="one", align_bytes=256)
         nc.gpsimd.memset(one[:], 1.0)
@@ -57,7 +57,6 @@ def tile_attend_tok_meanact_topk_kernel(tc, qT, k_words, k_scales, nb, offs, out
 
         ident = keep.tile([P, P], F32, name="ident", align_bytes=256)
         make_identity(nc, ident[:])
-        nc.gpsimd.memset(bias_pool[0:BIAS_ROW, T // 2 : T], 0.0)
 
         bias_rows = keep.tile([P, N], F32, name="bias_rows", align_bytes=256)
         nc.scalar.activation(out=bias_rows[:], in_=bias_pool[:].indirect(offsets[:]), func=ACT.Copy)

@@ -73,20 +73,23 @@ def tile_attend_tok_meanact_topk_kernel(tc, qT, k_words, k_scales, nb, offs, out
         q_last = keep.tile([P, PACK, QUARTER], F32, name="q_last", tag="scales_then_last_q", align_bytes=256)
         nc.sync.dma_start(out=q_last[:], in_=q_rows[:, :, HALF + QUARTER : NQ])
 
-        def quantize(name, raw, width, share, grouped_tag, plane_tag):
+        def gpsimd_cast(dst, src):
+            nc.gpsimd.tensor_scalar(dst, src, 1.0, 0.0, ALU.mult, ALU.add)
+
+        def quantize(name, raw, width, share, rest, grouped_tag, plane_tag):
             grouped = keep.tile([P, width, PACK], BF16, name="grouped_" + name, tag=grouped_tag, align_bytes=256)
             dst = lambda c0, c1: grouped[:, c0:c1, :].rearrange("p (c i) t -> p c t i", i=4)
             src = lambda c0, c1: raw[:, :, c0:c1].rearrange("p t (c i) -> p c t i", i=4)
             if share > 0:
                 nc.scalar.copy(out=dst(0, share), in_=src(0, share))
             if share < width:
-                nc.vector.tensor_copy(out=dst(share, width), in_=src(share, width))
+                rest(dst(share, width), src(share, width))
             code = keep.tile([P, width], U32, name="code_" + name, align_bytes=256)
             plane = keep.tile([P, width], U8, name="plane_" + name, tag=plane_tag, align_bytes=256)
             nc.vector.quantize_mx(out=code[:].bitcast(FP8X4), scales=plane[:], in_=grouped[:].rearrange("p w t -> p (w t)"))
             return code, plane
 
-        half = quantize("half", q_half, HALF, 0, "grouped_half", "plane_half")
+        half = quantize("half", q_half, HALF, 0, nc.vector.tensor_copy, "grouped_half", "plane_half")
 
         bias = keep.tile([P, TILES], F32, name="bias", align_bytes=256)
         nc.scalar.activation(out=bias[:], in_=bias_turned[:, :, BIAS_ROW], func=ACT.Copy, scale=mean_factor[:])
@@ -98,8 +101,8 @@ def tile_attend_tok_meanact_topk_kernel(tc, qT, k_words, k_scales, nb, offs, out
                 in_=word_pool[:].bitcast(U32).indirect(offsets[:, h * 16 : (h + 1) * 16]),
             )
 
-        third = quantize("third", q_third, QUARTER, QUARTER, "bias_then_grouped", "words_then_plane")
-        last = quantize("last", q_last, QUARTER, 0, "grouped_last", "plane_last")
+        third = quantize("third", q_third, QUARTER, 88, gpsimd_cast, "bias_then_grouped", "words_then_plane")
+        last = quantize("last", q_last, QUARTER, 0, nc.vector.tensor_copy, "grouped_last", "plane_last")
 
         active = keep.tile([P, TILES, RUNS, SEG], F32, name="active", align_bytes=256)
         means = keep.tile([P, TILES, RUNS], F32, name="means", align_bytes=256)

@@ -40,7 +40,7 @@ def tile_attend_tok_meanact_topk_kernel(tc, qT, k_words, k_scales, nb, offs, out
         scale_pool = keep.tile([P, T // 4], I32, name="scale_pool", tag="scales_then_last_q", align_bytes=256)
         nc.vector.memset(scale_pool[0:48, :], 0)
         nc.vector.memset(scale_pool[64:P, :], 0)
-        nc.sync.dma_start(out=scale_pool[48:64, :], in_=k_scales[0].bitcast(I32))
+        nc.scalar.dma_start(out=scale_pool[48:64, :], in_=k_scales[0].bitcast(I32))
         nc.scalar.dma_start(out=bias_pool[BIAS_ROW:P, :], in_=nb[0:1, :])
         one = keep.tile([P, 1], F32, name="one", align_bytes=256)
         nc.gpsimd.memset(one[:], 1.0)

@@ -35,6 +35,8 @@ def tile_attend_tok_meanact_topk_kernel(tc, qT, k_words, k_scales, nb, offs, out
         offsets = keep.tile([P, N // 16], U16, name="offsets")
         nc.sync.dma_start(offsets[:], offs)
 
+        one = keep.tile([P, 1], F32, name="one", align_bytes=256)
+        nc.vector.memset(one[:], 1.0)
         bias_pool = keep.tile([P, T], F32, name="bias_pool", tag="bias_then_grouped", align_bytes=256)
         nc.vector.memset(bias_pool[0:BIAS_ROW, :], 0.0)
         scale_pool = keep.tile([P, T // 4], I32, name="scale_pool", tag="scales_then_last_q", align_bytes=256)
@@ -42,8 +44,6 @@ def tile_attend_tok_meanact_topk_kernel(tc, qT, k_words, k_scales, nb, offs, out
         nc.vector.memset(scale_pool[64:P, :], 0)
         nc.scalar.dma_start(out=scale_pool[48:64, :], in_=k_scales[0].bitcast(I32))
         nc.scalar.dma_start(out=bias_pool[BIAS_ROW:P, :], in_=nb[0:1, :])
-        one = keep.tile([P, 1], F32, name="one", align_bytes=256)
-        nc.gpsimd.memset(one[:], 1.0)
         mean_factor = keep.tile([P, 1], F32, name="mean_factor", align_bytes=256)
         nc.scalar.activation(out=mean_factor[:], in_=one[:], func=ACT.Copy, scale=1.0 / SEG)
 
@@ -56,7 +56,8 @@ def tile_attend_tok_meanact_topk_kernel(tc, qT, k_words, k_scales, nb, offs, out
         nc.sync.dma_start(out=q_third[:], in_=q_rows[:, :, HALF : HALF + QUARTER])
 
         ident = keep.tile([P, P], F32, name="ident", align_bytes=256)
-        make_identity(nc, ident[:])
+        nc.vector.memset(ident[:], 0.0)
+        make_identity(nc, ident[:], nomemset=True)
 
         bias_rows = keep.tile([P, N], F32, name="bias_rows", align_bytes=256)
         nc.scalar.activation(out=bias_rows[:], in_=bias_pool[:].indirect(offsets[:]), func=ACT.Copy)

from contextlib import ExitStack

import concourse.mybir as mybir
from concourse.masks import make_identity

N, T, D, NQ, SEG = 512, 2048, 512, 512, 32
FLOPS = 2 * N * D * NQ
P = 128
PACK = 4
TILES = N // P
RUNS = NQ // SEG

F32 = mybir.dt.float32
BF16 = mybir.dt.bfloat16
I32 = mybir.dt.int32
U32 = mybir.dt.uint32
U16 = mybir.dt.uint16
U8 = mybir.dt.uint8
FP8X4 = mybir.dt.float8_e4m3fn_x4
ACT = mybir.ActivationFunctionType
ALU = mybir.AluOpType
AX = mybir.AxisListType

BIAS_ROW = P - 1
HALF = NQ // 2
QUARTER = NQ // 4


def tile_attend_tok_meanact_topk_kernel(tc, qT, k_words, k_scales, nb, offs, out):
    nc = tc.nc
    with ExitStack() as ctx:
        keep = ctx.enter_context(tc.tile_pool(name="keep", bufs=1))
        psum = ctx.enter_context(tc.psum_pool(name="psum", bufs=1))

        offsets = keep.tile([P, N // 16], U16, name="offsets")
        nc.sync.dma_start(offsets[:], offs)

        one = keep.tile([P, 1], F32, name="one", align_bytes=256)
        nc.vector.memset(one[:], 1.0)
        bias_pool = keep.tile([P, T], F32, name="bias_pool", tag="bias_then_grouped", align_bytes=256)
        nc.vector.memset(bias_pool[0:BIAS_ROW, :], 0.0)
        scale_pool = keep.tile([P, T // 4], I32, name="scale_pool", tag="scales_then_last_q", align_bytes=256)
        nc.vector.memset(scale_pool[0:48, :], 0)
        nc.vector.memset(scale_pool[64:P, :], 0)
        nc.scalar.dma_start(out=scale_pool[48:64, :], in_=k_scales[0].bitcast(I32))
        nc.scalar.dma_start(out=bias_pool[BIAS_ROW:P, :], in_=nb[0:1, :])
        mean_factor = keep.tile([P, 1], F32, name="mean_factor", align_bytes=256)
        nc.scalar.activation(out=mean_factor[:], in_=one[:], func=ACT.Copy, scale=1.0 / SEG)

        q_rows = qT[0].rearrange("(p j) w -> p j w", j=PACK)
        q_half = keep.tile([P, PACK, HALF], F32, name="q_half", align_bytes=256)
        nc.sync.dma_start(out=q_half[:], in_=q_rows[:, :, 0:HALF])
        word_pool = keep.tile([P, T], I32, name="word_pool", tag="words_then_plane", align_bytes=256)
        nc.sync.dma_start(out=word_pool[:], in_=k_words[0].rearrange("p n t -> p (n t)").bitcast(I32))
        q_third = keep.tile([P, PACK, QUARTER], F32, name="q_third", align_bytes=256)
        nc.sync.dma_start(out=q_third[:], in_=q_rows[:, :, HALF : HALF + QUARTER])

        ident = keep.tile([P, P], F32, name="ident", align_bytes=256)
        nc.vector.memset(ident[:], 0.0)
        make_identity(nc, ident[:], nomemset=True)

        bias_rows = keep.tile([P, N], F32, name="bias_rows", align_bytes=256)
        nc.scalar.activation(out=bias_rows[:], in_=bias_pool[:].indirect(offsets[:]), func=ACT.Copy)
        bias_turned = psum.tile([P, TILES, P], F32, name="bias_turned", tag="bank7")
        for m in range(TILES):
            nc.tensor.transpose(bias_turned[:, m, :], bias_rows[:, m * P : (m + 1) * P], ident[:])

        scale_picked = keep.tile([P, N], U8, name="scale_picked", align_bytes=256)
        nc.vector.tensor_copy(out=scale_picked[:], in_=scale_pool[:].bitcast(U8).indirect(offsets[:]))
        k_scale_words = keep.tile([P, N // 4], I32, name="k_scale_words", align_bytes=256)
        for r in range(4):
            nc.sync.dma_start(out=k_scale_words[r:P:32, :], in_=scale_picked[48 + r : 64 : 4, :].bitcast(I32))
        k_scale = k_scale_words[:].bitcast(U8)
        q_last = keep.tile([P, PACK, QUARTER], F32, name="q_last", tag="scales_then_last_q", align_bytes=256)
        nc.sync.dma_start(out=q_last[:], in_=q_rows[:, :, HALF + QUARTER : NQ])

        def gpsimd_cast(dst, src):
            nc.gpsimd.tensor_scalar(dst, src, 1.0, 0.0, ALU.mult, ALU.add)

        def quantize(name, raw, width, share, rest, grouped_tag, plane_tag):
            grouped = keep.tile([P, width, PACK], BF16, name="grouped_" + name, tag=grouped_tag, align_bytes=256)
            dst = lambda c0, c1: grouped[:, c0:c1, :].rearrange("p (c i) t -> p c t i", i=4)
            src = lambda c0, c1: raw[:, :, c0:c1].rearrange("p t (c i) -> p c t i", i=4)
            if share > 0:
                nc.scalar.copy(out=dst(0, share), in_=src(0, share))
            if share < width:
                rest(dst(share, width), src(share, width))
            code = keep.tile([P, width], U32, name="code_" + name, align_bytes=256)
            plane = keep.tile([P, width], U8, name="plane_" + name, tag=plane_tag, align_bytes=256)
            nc.vector.quantize_mx(out=code[:].bitcast(FP8X4), scales=plane[:], in_=grouped[:].rearrange("p w t -> p (w t)"))
            return code, plane

        half = quantize("half", q_half, HALF, 0, nc.vector.tensor_copy, "grouped_half", "plane_half")

        bias = keep.tile([P, TILES], F32, name="bias", align_bytes=256)
        nc.scalar.activation(out=bias[:], in_=bias_turned[:, :, BIAS_ROW], func=ACT.Copy, scale=mean_factor[:])

        k_code = keep.tile([P, N], U32, name="k_code", align_bytes=256)
        for h in range(2):
            nc.vector.tensor_copy(
                out=k_code[:, h * 256 : (h + 1) * 256],
                in_=word_pool[:].bitcast(U32).indirect(offsets[:, h * 16 : (h + 1) * 16]),
            )

        third = quantize("third", q_third, QUARTER, 88, gpsimd_cast, "bias_then_grouped", "words_then_plane")
        last = quantize("last", q_last, QUARTER, 0, nc.vector.tensor_copy, "grouped_last", "plane_last")

        active = keep.tile([P, TILES, RUNS, SEG], F32, name="active", align_bytes=256)
        means = keep.tile([P, TILES, RUNS], F32, name="means", align_bytes=256)
        out_view = out[0].rearrange("(m p) j -> p m j", p=P)

        def product(index, part, first_run, m, j0, j1, accumulated=0):
            code, plane = part
            cols = slice((j0 - first_run) * SEG, (j1 - first_run) * SEG)
            acc = psum.tile([P, j1 - j0, SEG], F32, name="acc%d" % index, tag="bank%d" % (index % 8))
            nc.tensor.matmul_mx(
                out=acc[:].rearrange("p j e -> p (j e)"),
                lhsT=k_code[:, m * P : (m + 1) * P].bitcast(FP8X4),
                lhsT_scale=k_scale[:, m * P : (m + 1) * P],
                rhs=code[:, cols].bitcast(FP8X4),
                rhs_scale=plane[:, cols],
                start=True,
                stop=True,
            )
            plain = j1 - accumulated
            if plain > j0:
                nc.scalar.activation(
                    out=active[:, m, j0:plain, :],
                    in_=acc[:, 0 : plain - j0, :],
                    func=ACT.Relu,
                    bias=bias[:, m : m + 1],
                    scale=1.0 / SEG,
                )
            for j in range(plain, j1):
                nc.scalar.activation(
                    out=active[:, m, j, :],
                    in_=acc[:, j - j0, :],
                    func=ACT.Relu,
                    bias=bias[:, m : m + 1],
                    scale=1.0 / SEG,
                    accum_out=means[:, m, j : j + 1],
                )

        def add_up(m0, m1, j0, j1):
            nc.vector.tensor_reduce(out=means[:, m0:m1, j0:j1], in_=active[:, m0:m1, j0:j1, :], axis=AX.X, op=ALU.add)

        def store(m0, m1):
            nc.sync.dma_start(out=out_view[:, m0:m1, :], in_=means[:, m0:m1, :])

        product(0, half, 0, 0, 0, 4)
        product(1, half, 0, 0, 4, 8)
        add_up(0, 1, 0, 8)
        product(2, half, 0, 1, 0, 8)
        product(3, half, 0, 2, 0, 8)
        add_up(1, 3, 0, 8)
        product(4, half, 0, 3, 0, 8)
        product(5, third, 8, 3, 8, 12)
        add_up(3, 4, 0, 12)
        for m in range(3):
            product(6 + m, third, 8, m, 8, 12)
        add_up(0, 3, 8, 12)
        for m in range(2):
            product(9 + m, last, 12, m, 12, 16)
        add_up(0, 2, 12, 16)
        store(0, 2)
        product(11, last, 12, 2, 12, 16)
        add_up(2, 3, 12, 16)
        product(12, last, 12, 3, 12, 16, accumulated=4)
        store(2, 3)
        store(3, 4)
